import numpy as np, ml_dtypes
CORES = [4,12,20,28,44,60,76,84,92,108,116,124]
N = 12
VB, TK = 1, 128
def setup_inputs(rng):
    h = rng.standard_normal((128, TK), dtype=np.float32) / 4; w = rng.standard_normal((N, 128, VB * 128), dtype=np.float32)
    a = 2 * np.pi * rng.random((TK)); s = 400 * rng.random((TK)) ** 1.5; h[0] = s * np.cos(a); h[1] = s * np.sin(a); h[2] = 150 * rng.standard_normal((TK)); w[:, 2, :] = 1 + w[:, 2, :] / 50
    a = (2 * np.pi * rng.random() + np.pi / 2 * (rng.permutation(N).reshape(N, 1, 1) + 0.5) / N - 0.5 + (np.arange(VB).reshape(1, VB, 1) + rng.random((N, VB, 128))) / VB).reshape(N, VB * 128); w[:, 0, :] = np.cos(a); w[:, 1, :] = np.sin(a)
    tgt = rng.integers(0, N * VB * 128, size=TK)
    oh = np.zeros((N * VB * 128, TK), np.float32); oh[tgt, np.arange(TK)] = 1.0
    oh = oh.reshape(N, VB, 128, TK).transpose(0, 2, 1, 3).reshape(N, 128, VB * TK)
    return {"h": np.broadcast_to(h, (N, 128, TK)).astype(ml_dtypes.bfloat16), "w": w.astype(ml_dtypes.bfloat16), "oh": oh.astype(ml_dtypes.bfloat16)}
def reference(h, w, oh):
    H, W, OH = h.astype(np.float64), w.astype(np.float64), oh.astype(np.float64)
    Z = np.concatenate([W[r].T @ H[r] for r in range(N)], axis=0)
    O = np.concatenate([OH[r][:, TK * b:TK * b + TK] for r in range(N) for b in range(VB)], axis=0)
    m = Z.max(axis=0)
    P = np.exp(Z - m); P = P / P.sum(axis=0)
    G = P - O
    d = sum(W[r] @ G[VB * 128 * r:VB * 128 * (r + 1)] for r in range(N)).astype(ml_dtypes.bfloat16)
    return {"d": np.broadcast_to(d, (N,) + d.shape)}

from concourse.bass import DstId, RemoteDMATransfer
from concourse.mybir import AluOpType, AxisListType, ActivationFunctionType

N = 12
NB = 8
SLOT = NB + 128 + 128 + NB
OA, OB, OS = NB, NB + 128, NB + 256

SCRATCH = {
    "w_sb": ("sbuf", [128, 128], "bfloat16"),
    "h_sb": ("sbuf", [128, 128], "bfloat16"),
    "oh_sb": ("sbuf", [128, 128], "bfloat16"),
    "dif": ("sbuf", [128, 128], "float32"),
    "sq": ("sbuf", [128, 128], "float32"),
    "ident": ("sbuf", [128, 128], "bfloat16"),
    "wT_sb": ("sbuf", [128, 128], "bfloat16"),
    "eT_sb": ("sbuf", [128, 128], "bfloat16"),
    "e_sb": ("sbuf", [128, 128], "bfloat16"),
    "land": ("sbuf", [128, N * SLOT], "bfloat16"),
    "diag": ("sbuf", [128, N * 128], "bfloat16"),
    "diagS": ("sbuf", [128, 128], "bfloat16"),
    "U_sb": ("sbuf", [128, 128], "bfloat16"),
    "d_sb": ("sbuf", [128, 128], "bfloat16"),
    "s32": ("sbuf", [128, 1], "float32"),
    "mn": ("sbuf", [128, 1], "float32"),
    "ecol": ("sbuf", [128, N], "float32"),
    "es": ("sbuf", [128, N], "float32"),
    "S": ("sbuf", [128, 1], "float32"),
    "rS": ("sbuf", [128, 1], "float32"),
    "z_ps": ("psum", [128, 512], "float32"),
    "A_ps": ("psum", [128, 512], "float32"),
    "B_ps": ("psum", [128, 512], "float32"),
    "U_ps": ("psum", [128, 512], "float32"),
    "d_ps": ("psum", [128, 512], "float32"),
    "wT_ps": ("psum", [128, 1024], "bfloat16"),
    "e_ps": ("psum", [128, 1024], "bfloat16"),
}
SEMAPHORES = (["ld_w", "ld_h", "ld_oh", "s_iota", "s_sq", "s_id", "s_pad", "s_z", "s_m", "s_wTp", "s_wT", "s_Bp",
               "s_B", "s_eT", "s_s", "s_ep", "s_e", "s_Ap", "s_A", "s_mn", "s_ec", "s_U", "s_es", "s_S", "s_rS",
               "s_dS", "s_Usb", "s_d", "s_dsb", "st", "loc"]
              + ["N%d" % r for r in range(N)] + ["P%d" % r for r in range(N)] + ["dg%d" % r for r in range(N)])

DIRECT = 3


def _bits(mask):
    return [i for i in range(mask.bit_length()) if (mask >> i) & 1]


def _mask_of(bits):
    m = 0
    for b in bits:
        m |= 1 << b
    return m


def _plan(cores, topo):
    plan = []
    for r, c in enumerate(cores):
        near = [q for q in range(N) if topo.may_write(c, cores[q])]
        far = [q for q in range(N) if not topo.may_write(c, cores[q])]
        j = near.index(r)
        near = near[j + 1:] + near[:j]
        carriers = [k for k in range(topo.CORES_PER_CHIP * topo.CHIPS)
                    if topo.chip(k) == topo.chip(c) and k != c and all(topo.may_write(k, x) for x in cores)]
        H = len(carriers)
        rest = near[DIRECT:]
        per = len(far) // H
        far = far[(per * j) % len(far):] + far[:(per * j) % len(far)]
        lists = [far[q * per:(q + 1) * per] for q in range(H)]
        for i, q in enumerate(far[per * H:] + rest):
            lists[i % H].append(q)
        plan.append((near[:DIRECT], [(carriers[q], lists[q]) for q in range(H) if lists[q]]))
    return plan


def _xfer(topo, src_core, dst_cores, ap, mask, sem):
    ids = []
    for k in dst_cores:
        rid, pid, _se = topo.addr(k)
        ids.append(DstId(rid=rid, pnc=pid))
    return RemoteDMATransfer(dst_ids=ids, dma_engine_mask=mask, remote_sem=sem, srcs=[ap],
                             dsts=[ap for _k in dst_cores], alu_op=0)


def rank_program(g, core, T, topo):
    cores = list(T.cores)
    plan = _plan(cores, topo)
    sem = T.sem
    land = T.land

    def blkN(r):
        return land[:, r * SLOT:r * SLOT + NB]

    def blkP(r):
        return land[:, r * SLOT + NB:(r + 1) * SLOT]

    rank = T.rank_of(core)
    if rank is None:
        for r in range(N):
            for k, dests in plan[r][1]:
                if k != core:
                    continue
                dst = [cores[q] for q in dests]
                m = topo.mask(core, dst[0])
                for x in dst:
                    m &= topo.mask(core, x)
                n_in = len(_bits(topo.mask(cores[r], core))) // len(plan[r][1])
                g.wait_ge(sem["N%d" % r], n_in)
                g.remote_dma_fused([_xfer(topo, core, dst, blkN(r), m, sem["N%d" % r])], local_sem=sem.loc)
                g.wait_ge(sem["P%d" % r], n_in)
                g.remote_dma_fused([_xfer(topo, core, dst, blkP(r), m, sem["P%d" % r])], local_sem=sem.loc)
                g.wait_ge(sem.loc, 2 * len(_bits(m)))
        return

    r0 = rank
    direct, carried = plan[r0]
    X = AxisListType.X
    Act = ActivationFunctionType
    v, pe, act, sy = g.vector, g.tensor, g.scalar, g.sync
    b0 = r0 * SLOT
    nm_own = land[:, b0:b0 + 1]
    nm_all = land[:, 0:N * SLOT:SLOT]
    s_all = land[:, OS:N * SLOT:SLOT]

    adds, when = {}, {}
    for r in range(N):
        if r == r0:
            continue
        if r0 in plan[r][0]:
            adds[r] = len(_bits(topo.mask(cores[r], core)))
            when[r] = (0, plan[r][0].index(r0))
        for k, dests in plan[r][1]:
            if r0 in dests:
                m = topo.mask(k, core)
                for q in dests:
                    m &= topo.mask(k, cores[q])
                adds[r] = len(_bits(m))
                when[r] = (1, dests.index(r0))
    order = [r0] + sorted(adds, key=lambda r: (when[r], r))

    sy.dma_start(T.w_sb[:], T.w[:]).then_inc(sem.ld_w, 16)
    act.dma_start(T.h_sb[:], T.h[:]).then_inc(sem.ld_h, 16)
    sy.dma_start(T.oh_sb[:], T.oh[:]).then_inc(sem.ld_oh, 16)

    g.iota(T.dif[:], [[-1, 128]], 0, 1, allow_small_or_imprecise_dtypes=True).then_inc(sem.s_iota, 1)
    act.wait_ge(sem.s_iota, 1)
    act.activation(T.sq[:], T.dif[:], Act.Square).then_inc(sem.s_sq, 1)
    act.wait_ge(sem.s_sq, 1)
    act.activation(T.ident[:], T.sq[:], Act.Exp, scale=-100.0).then_inc(sem.s_id, 1)
    v.memset(land[:, b0 + 1:b0 + NB], 0.0).then_inc(sem.s_pad, 1)
    v.memset(land[:, b0 + OS + 1:b0 + SLOT], 0.0).then_inc(sem.s_pad, 1)

    pe.wait_ge(sem.ld_w, 16)
    pe.wait_ge(sem.ld_h, 16)
    pe.matmul(T.z_ps[:, 0:128], T.h_sb[:], T.w_sb[:], True, True).then_inc(sem.s_z, 1)
    pe.wait_ge(sem.s_id, 1)
    pe.transpose(T.wT_ps[:, 0:128], T.w_sb[:], T.ident[:]).then_inc(sem.s_wTp, 1)

    v.wait_ge(sem.s_z, 1)
    v.tensor_reduce(nm_own, T.z_ps[:, 0:128], X, AluOpType.max, negate=True).then_inc(sem.s_m, 1)
    v.wait_ge(sem.s_wTp, 1)
    v.tensor_copy(T.wT_sb[:], T.wT_ps[:, 0:128]).then_inc(sem.s_wT, 1)

    act.wait_ge(sem.s_m, 1)
    act.activation(T.eT_sb[:], T.z_ps[:, 0:128], Act.Exp, bias=nm_own, scale=1.0,
                   accum_out=T.s32[:]).then_inc(sem.s_eT, 1)

    pe.wait_ge(sem.s_eT, 1)
    pe.transpose(T.e_ps[:, 0:128], T.eT_sb[:], T.ident[:]).then_inc(sem.s_ep, 1)
    pe.wait_ge(sem.s_wT, 1)
    pe.wait_ge(sem.ld_oh, 16)
    pe.matmul(T.B_ps[:, 0:128], T.oh_sb[:], T.wT_sb[:], True, True).then_inc(sem.s_Bp, 1)
    pe.wait_ge(sem.s_e, 1)
    pe.matmul(T.A_ps[:, 0:128], T.e_sb[:], T.wT_sb[:], True, True).then_inc(sem.s_Ap, 1)

    v.wait_ge(sem.s_eT, 1)
    v.tensor_copy(land[:, b0 + OS:b0 + OS + 1], T.s32[:]).then_inc(sem.s_s, 1)
    v.wait_ge(sem.s_ep, 1)
    v.tensor_copy(T.e_sb[:], T.e_ps[:, 0:128]).then_inc(sem.s_e, 1)
    act.wait_ge(sem.s_Bp, 1)
    act.activation(land[:, b0 + OB:b0 + OB + 128], T.B_ps[:, 0:128], Act.Copy, scale=-1.0).then_inc(sem.s_B, 1)
    v.wait_ge(sem.s_Ap, 1)
    v.tensor_copy(land[:, b0 + OA:b0 + OA + 128], T.A_ps[:, 0:128]).then_inc(sem.s_A, 1)

    on_bits = _bits(topo.mask(core, carried[0][0]))
    share = len(on_bits) // len(carried)
    off_mask = topo.mask(core, cores[direct[0]])
    sent = 0

    def hand_over(ap, s):
        g.remote_dma_fused([_xfer(topo, core, [k], ap, _mask_of(on_bits[i * share:(i + 1) * share]), s)
                            for i, (k, _d) in enumerate(carried)], local_sem=sem.loc)
        return share * len(carried)

    g.wait_ge(sem.s_m, 1)
    g.wait_ge(sem.s_pad, 2)
    sent += hand_over(blkN(r0), sem["N%d" % r0])
    g.wait_ge(sem.s_A, 1)
    g.wait_ge(sem.s_B, 1)
    g.wait_ge(sem.s_s, 1)
    sent += hand_over(blkP(r0), sem["P%d" % r0])
    dcores = [cores[q] for q in direct]
    g.remote_dma_fused([_xfer(topo, core, dcores, blkN(r0), off_mask, sem["N%d" % r0])], local_sem=sem.loc)
    g.remote_dma_fused([_xfer(topo, core, dcores, blkP(r0), off_mask, sem["P%d" % r0])], local_sem=sem.loc)
    sent += 2 * len(_bits(off_mask))
    g.wait_ge(sem.loc, sent)

    v.wait_ge(sem.s_m, 1)
    for r in order[1:]:
        v.wait_ge(sem["N%d" % r], adds[r])
    v.tensor_reduce(T.mn[:], nm_all, X, AluOpType.min).then_inc(sem.s_mn, 1)
    act.wait_ge(sem.s_mn, 1)
    act.activation(T.ecol[:], nm_all, Act.Exp, bias=T.mn[:], scale=-1.0).then_inc(sem.s_ec, 1)
    v.wait_ge(sem.s_ec, 1)
    v.wait_ge(sem.s_id, 1)
    for r in order:
        v.tensor_scalar(T.diag[:, r * 128:(r + 1) * 128], T.ident[:], T.ecol[:, r:r + 1], None,
                        AluOpType.mult).then_inc(sem["dg%d" % r], 1)

    pe.wait_ge(sem.s_A, 1)
    pe.wait_ge(sem.s_B, 1)
    for i, r in enumerate(order):
        b = r * SLOT
        if r != r0:
            pe.wait_ge(sem["P%d" % r], adds[r])
        pe.matmul(T.d_ps[:, 0:128], land[:, b + OB:b + OB + 128], T.ident[:], i == 0, False)
        pe.wait_ge(sem["dg%d" % r], 1)
        mm = pe.matmul(T.U_ps[:, 0:128], T.diag[:, r * 128:(r + 1) * 128], land[:, b + OA:b + OA + 128],
                       i == 0, i == N - 1)
        if i == N - 1:
            mm.then_inc(sem.s_U, 1)

    v.wait_ge(sem.s_s, 1)
    for r in order[1:]:
        v.wait_ge(sem["P%d" % r], adds[r])
    v.tensor_tensor(T.es[:], T.ecol[:], s_all, AluOpType.mult).then_inc(sem.s_es, 1)
    v.wait_ge(sem.s_es, 1)
    v.tensor_reduce(T.S[:], T.es[:], X, AluOpType.add).then_inc(sem.s_S, 1)
    v.wait_ge(sem.s_S, 1)
    v.reciprocal(T.rS[:], T.S[:]).then_inc(sem.s_rS, 1)
    v.wait_ge(sem.s_rS, 1)
    v.tensor_scalar(T.diagS[:], T.ident[:], T.rS[:], None, AluOpType.mult).then_inc(sem.s_dS, 1)

    act.wait_ge(sem.s_U, 1)
    act.activation(T.U_sb[:], T.U_ps[:, 0:128], Act.Copy).then_inc(sem.s_Usb, 1)

    pe.wait_ge(sem.s_Usb, 1)
    pe.wait_ge(sem.s_dS, 1)
    pe.matmul(T.d_ps[:, 0:128], T.U_sb[:], T.diagS[:], False, True).then_inc(sem.s_d, 1)
    v.wait_ge(sem.s_d, 1)
    v.tensor_copy(T.d_sb[:], T.d_ps[:, 0:128]).then_inc(sem.s_dsb, 1)
    sy.wait_ge(sem.s_dsb, 1)
    sy.dma_start(T.d[:], T.d_sb[:]).then_inc(sem.st, 16)
    sy.wait_ge(sem.st, 16)
